import numpy as np, ml_dtypes
CORES = [2,3,42,43,82,83,122,123]
N = 8
import mx_ref
BF = ml_dtypes.bfloat16
def gentries(a):
    return np.ascontiguousarray(a.reshape(8, 16, -1).transpose(0, 2, 1)).reshape(8, -1)
def gtable(e):
    e = np.asarray(e); return np.ascontiguousarray(e.reshape(8, -1, 16).transpose(0, 2, 1)).reshape(128, -1).astype(np.int32)
def gcols(t, e):
    v = np.concatenate([t.reshape(8, 16, -1, 4), np.zeros((8, 16, 1, 4), BF)], axis=2)
    return np.ascontiguousarray(np.stack([v[g][:, e[g]] for g in range(8)])).reshape(128, -1)
def tile(rs):
    return np.stack(rs, axis=2).reshape(128, -1).astype(BF)
def pick(q, e):
    c = np.concatenate([q[0].reshape(128, -1, 4), np.zeros((128, 1, 4), np.uint8)], axis=1); s = np.concatenate([q[1], np.ones((16, 1), np.uint8)], axis=1)
    return (np.ascontiguousarray(c[:, e].reshape(128, -1)), np.ascontiguousarray(s[:, e]))
def join(*qs):
    return (np.concatenate([q[0] for q in qs], axis=1), np.concatenate([q[1] for q in qs], axis=1))
def put(q, e, v):
    c, s = q[0].reshape(128, -1, 4).copy(), q[1].copy(); c[:, e] = v[0].reshape(128, -1, 4); s[:, e] = v[1]
    return (c.reshape(128, -1), s)
def pk(c, s):
    return (np.ascontiguousarray(c), mx_ref.live(s))
def emit(q):
    return q[0], q[1]
def packed(v, rng):
    q = [mx_ref.quantize(np.ascontiguousarray(v[r])) for r in range(N)]
    return np.stack([a for a, b in q]), np.stack([mx_ref.plane(b, rng) for a, b in q])
def values_of_codes():
    e, c = np.zeros((128, 128, 4), np.float32), np.zeros((128, 2, 4), np.uint8)
    e[np.arange(128), np.arange(128), 0] = 1
    c[:127, :, 0] = np.arange(256).reshape(2, 128).T[:127]
    return mx_ref.matmul(mx_ref.quantize(e.reshape(128, 512).astype(BF)), (c.reshape(128, 8), np.full((16, 2), 127, np.uint8))).T.reshape(-1).astype(np.float64)
CODE_VALUE, SCALE_VALUE = values_of_codes(), 2.0 ** (np.arange(256) - 127.0)
def decode(q):
    return (CODE_VALUE[q[0]].reshape(16, 8, -1, 4) * SCALE_VALUE[q[1]][:, None, :, None] + 0.0).reshape(128, -1).astype(np.float32)
def f(rng, *shape):
    return mx_ref.flush((rng.standard_normal(shape, dtype=np.float32) * np.exp2(rng.integers(-2, 3, shape[:-1] + (1,)))).astype(BF))
def wide(rng, *shape, cols=0):
    v = rng.standard_normal(shape, dtype=np.float32) * np.exp2(rng.integers(-12, 13, shape)).astype(np.float32)
    if cols: v *= np.repeat(np.exp2(rng.integers(-cols, cols + 1, shape[:-2] + (1, shape[-1] // 4))) * (rng.random(shape[:-2] + (1, shape[-1] // 4)) > 0.0625), 4, axis=-1).astype(np.float32)
    return mx_ref.flush(v.astype(BF))
C, HALF, FAR = 384, 192, (1, 4)
def mate(r, t):
    return r ^ FAR[t]
def swap(s, t):
    lo, hi = np.arange(HALF), np.arange(HALF, C)
    return [join(pick(s[r], lo), pick(s[mate(r, t)], hi)) for r in range(N)]
def contend(e, p):
    a, b = p[:, ::2], p[:, 1::2]
    w = np.take_along_axis(e, b, axis=1) > np.take_along_axis(e, a, axis=1)
    l = np.empty_like(p)
    l[:, ::2] = np.where(w, b, a)
    l[:, 1::2] = np.where(w, a, b)
    return l
def layer(w, q):
    return [mx_ref.matmul(pick(w, np.arange(128 * b, 128 * b + 128)), q) for b in range(4)]
def clean(v):
    v = v.astype(np.float32)
    v[np.abs(v) < np.float32(2.0 ** -16)] = 0
    return v.astype(BF)
def numbers_of(rng):
    return {"x": clean(f(rng, N, 128, 4 * C)), "u": np.array(f(rng, N, 128, 512)), "v": np.array(f(rng, N, 128, 512))}
def wirings(rng):
    return {k: np.stack([gtable(np.stack([rng.permutation(C) for g in range(8)])) for r in range(N)]) for k in ("p0", "p1")}
def layers(rng, w, z):
    wc, ws = packed(np.stack([w] * N), rng)
    zc, zs = packed(np.stack([z] * N), rng)
    return {"wc": wc, "ws": ws, "zc": zc, "zs": zs}
def still(rng, k=1.0):
    w = np.zeros((128, 4, 128, 4), np.float32)
    i = np.arange(128)
    for b in range(4): w[i, b, i, b] = 32
    w = w.reshape(128, 2048)
    return layers(rng, w.astype(BF), (w * np.float32(k)).astype(BF))
def signs(rng):
    return np.stack([rng.permutation(8) % 2 * 2.0 - 1.0 for r in range(N)])
def pairs(rng, o):
    w = []
    for g in range(8):
        k = o[g].reshape(HALF, 2)[rng.permutation(HALF)]
        w.append(np.where(rng.integers(0, 2, (HALF, 1)) == 1, k[:, ::-1], k).reshape(-1))
    return np.stack(w)
def setup_inputs(rng):
    return {**numbers_of(rng), **wirings(rng), **layers(rng, np.array(f(rng, 128, 2048)), np.array(f(rng, 128, 2048)))}
def setup_inputs_ties(rng):
    d = numbers_of(rng)
    e = int(rng.integers(N))
    x = d["x"].reshape(N, 8, 16, C, 4)
    a = x[0][:, :8, :3].copy()
    a[:, :, 2] = 0
    for r in range(N):
        k = np.zeros(C, int) if r in (e, mate(e, 0)) else rng.permutation(C) % 3
        x[r][:, :8] = a[:, :, k]
    x[mate(e, 1)] = 0
    u = d["u"].reshape(N, 8, 16, 128, 4)
    for t in range(2): u[:, :, 8:, t::16] = 0
    w = np.array(f(rng, 128, 2048)).reshape(8, 16, 4, 8, 16, 4)
    w[:, 8:, :, :, :8] = 0
    return {"x": x.reshape(N, 128, 4 * C), "u": u.reshape(N, 128, 512), "v": d["v"], **wirings(rng), **layers(rng, w.reshape(128, 2048), np.array(f(rng, 128, 2048)))}
def setup_inputs_near(rng):
    d = numbers_of(rng)
    x = d["x"].astype(np.float32).reshape(N, 8, 16, C, 4)
    s = np.arange(C) // 2
    g = ((s[:, None] >> np.arange(8)) & 1) * np.exp2(np.arange(8) - 22.0)
    x[:, :, 0] = 0
    x[:, :, 0, :, 0] = 1
    x[:, :, 8] = g[:, :4]
    x[:, :, 9] = g[:, 4:]
    x[:, :, 10:] = rng.integers(4, 8, (N, 8, 6, C, 4)) * rng.choice([-1.0, 1.0], (N, 8, 6, C, 4)) * 2.0 ** -20
    one = int(rng.integers(8))
    x[:, one, 1:8] = 0
    x[:, one, 1, :, 0] = 1.75
    x[:, one, 2:4] = np.exp2(-np.arange(11.0, 19.0)).reshape(2, 1, 4)
    u = d["u"].reshape(N, 128, 128, 4)
    for t in range(2):
        u[:, :, t::16] = 0
        c = np.stack([np.exp2(-4.0 * rng.permutation(8)) for r in range(N)])
        k = (signs(rng) * c).astype(np.float32).astype(BF)
        c = c.astype(np.float32).astype(BF)
        for h in range(8):
            u[:, 16 * h, 16 * h + t, 0] = k[:, h]
            u[:, 16 * h + 8:16 * h + 10, 16 * h + t] = c[:, h][:, None, None]
    first = [pairs(rng, np.stack([np.roll(np.arange(C), -int(k)) for k in rng.permutation(8) % 2])) for r in range(N)]
    mixed = [s[contend(np.tile(s, (8, 1)), first[r])] + s for r in range(N)]
    second = []
    for r in range(N):
        k = np.concatenate([mixed[r][:, :HALF], mixed[mate(r, 1)][:, HALF:]], axis=1)
        second.append(pairs(rng, np.argsort(k, axis=1, kind="stable")))
    return {"x": x.reshape(N, 128, 4 * C).astype(BF), "u": u.reshape(N, 128, 512), "v": d["v"], "p0": np.stack([gtable(k) for k in first]), "p1": np.stack([gtable(k) for k in second]), **still(rng, 1.125)}
def setup_inputs_huge(rng):
    d = numbers_of(rng)
    x = 2.0 ** 30 * (0.6 + 0.4 * rng.random((N, 128, 4 * C)))
    u = d["u"].reshape(N, 128, 128, 4)
    for t in range(2):
        a = 2.0 ** 30 * (1 - 0.25 * rng.random((N, 128, 8, 4))) * signs(rng)[:, None, :, None]
        u[:, :, t::16] = a.astype(np.float32).astype(BF)
    return {"x": x.astype(np.float32).astype(BF), "u": u.reshape(N, 128, 512), "v": d["v"], **wirings(rng), **still(rng)}
def setup_inputs_spread(rng):
    d = setup_inputs(rng)
    d["x"] = clean(wide(rng, N, 128, 4 * C, cols=10))
    return d
def check_inputs(d):
    b = []
    for k in ("x", "u", "v"):
        a = np.abs(d[k].astype(np.float32))
        if not (np.isfinite(a).all() and ((a == 0) | (a >= 2.0 ** -30) & (a <= 2.0 ** 30)).all()): b.append("a value of " + k)
    for k in ("p0", "p1"):
        if any((np.sort(gentries(a), axis=1) != np.arange(C)).any() for a in d[k]): b.append("a group of " + k + " hasn't every number once")
    for k in ("wc", "zc"):
        if (d[k] != d[k][:1]).any(): b.append(k + " differs between ranks")
    for k in ("ws", "zs"):
        s = [mx_ref.live(p) for p in d[k]]
        if any((p != s[0]).any() for p in s): b.append(k + " differs between ranks")
    return b
def reference(x, u, v, p0, p1, wc, ws, zc, zs):
    w, z = pk(wc[0], ws[0]), pk(zc[0], zs[0])
    qu = [mx_ref.quantize(u[r]) for r in range(N)]
    now = [mx_ref.quantize(x[r]) for r in range(N)]
    kept = [[], []]
    for t in range(2):
        now = swap(now, t)
        for r in range(N):
            e = mx_ref.matmul(qu[r], now[r])[t::16] + np.float32(0.0)
            l = contend(e, gentries((p0, p1)[t][r]))
            kept[t].append(l)
            d = decode(now[r])
            p = ((gcols(d.astype(BF), l).astype(np.float32) + d) * np.float32(0.5)).astype(BF)
            now[r] = mx_ref.quantize(tile([np.maximum(a, np.float32(0.0)) * np.float32(0.03125) for a in layer(w, mx_ref.quantize(p))]))
    for t in (1, 0):
        for r in range(N):
            g = tile([a * np.float32(0.03125) for a in layer(z, now[r])])
            now[r] = mx_ref.quantize(gcols(g, np.argsort(kept[t][r], axis=1)))
        now = swap(now, t)
    y, ol = np.zeros((N, 128, C), np.float32), np.zeros((N, 8, 2 * C), np.float32)
    oc, osc = np.zeros((N, 128, 4 * C), np.uint8), np.zeros((N, 16, C), np.uint8)
    for r in range(N):
        y[r] = mx_ref.matmul(mx_ref.quantize(v[r]), now[r])
        ol[r] = np.concatenate([kept[0][r], kept[1][r]], axis=1)
        oc[r], osc[r] = emit(now[r])
    return {"y": y, "ol": ol, "oc": oc, "osc": osc}

@@ -1,0 +1,333 @@
+from concourse.mybir import dt, AluOpType, ActivationFunctionType
+
+A = AluOpType
+COPY, RELU = ActivationFunctionType.Copy, ActivationFunctionType.Relu
+C, HALF, FAR = 384, 192, (1, 4)
+SCALE = 0.03125
+ENGINES = (8, 8, 8, 8)
+F8, U8, BF, F32, I32, U16 = "float8_e4m3fn_x4", "uint8", "bfloat16", "float32", "int32", "uint16"
+
+SCRATCH = {"ps": ("psum", [128, 4096], F32)}
+
+
+def _buf(dtype, **shapes):
+    for k, n in shapes.items():
+        SCRATCH[k] = ("sbuf", [128, n], dtype)
+
+
+def _mx(**widths):
+    for k, n in widths.items():
+        SCRATCH[k] = ("sbuf", [128, n], F8)
+        SCRATCH[k + "s"] = ("sbuf", [128, n], U8)
+
+
+_buf(BF, xt=4 * C, ut=512, vt=512, eb=520)
+_buf(F32, idn=128, j8=HALF, iot=C, phf=1, sel=C, keep=C, w48=96, c48=96, cf=96, f24=96, f383=96, ff=96, yt=C)
+_buf(I32, pt=96, ipp=1, phi=1, uoi=16, fsh=96)
+_buf(U16, uof=16, pu=48)
+_mx(eq=512, uq=128, up=256, vq=128, wq=512, zq=512, fin=C)
+for _t in "01":
+    _buf(F32, **{k + _t: n for k, n in dict(sc=C, mm=C, rr=C, ll=48, lf=48, inv=C, ivw=24, lr=C).items()})
+    _buf(U16, **{k + _t: 24 for k in ("lu", "fu", "iu")})
+    _buf(BF, **{k + _t: n for k, n in dict(dd=4 * C, de=2 * C, gt=4 * C, pm=4 * C, hh=4 * C, gg=4 * C, xx=4 * C).items()})
+    _mx(**{k + _t: n for k, n in dict(st=C, qp=C, su=HALF, bu=HALF).items()})
+_mx(sb=C, s2=C)
+
+NDMA = 24
+SEMAPHORES = ["qv", "qa", "qt", "qg"] + ["r%d" % k for k in range(4)] + ["l%d" % k for k in range(4)] + ["d%d" % k for k in range(NDMA)]
+
+
+def rank_program(g, core, T, topo):
+    me = T.rank_of(core)
+    if me is None:
+        return
+    queues = {"v": g.vector, "a": g.scalar, "t": g.tensor, "g": g, "s": g.sync}
+    count, seen, dmas = {"v": 0, "a": 0, "t": 0, "g": 0}, {}, []
+
+    def wait(q, deps):
+        need = {}
+        for s, n in deps:
+            need[s] = max(n, need.get(s, 0))
+        for s, n in need.items():
+            if seen.get((q, s), 0) < n:
+                queues[q].wait_ge(T.sem[s], n)
+                seen[(q, s)] = n
+
+    def op(q, deps, call, *args, **kw):
+        wait(q, deps)
+        call(*args, **kw).then_inc(T.sem["q" + q], 1)
+        count[q] += 1
+        return ("q" + q, count[q])
+
+    def dma(q, deps, *moves):
+        wait(q, deps)
+        s = "d%d" % len(dmas)
+        for out, in_ in moves:
+            queues[q].dma_start(out, in_).then_inc(T.sem[s], 16)
+        dmas.append((s, 16 * len(moves)))
+        return dmas[-1]
+
+    V, S, P = g.vector, g.scalar, g.tensor
+    readers = {b: [] for b in range(8)}
+
+    def bank(b, n=HALF):
+        return T.ps[:, 512 * b:512 * b + n]
+
+    def mm(b, w, c0, x, a, n, deps):
+        t = op("t", deps + readers[b], P.matmul_mx, bank(b, n), T[w][:, c0:c0 + 128], T[w + "s"][:, c0:c0 + 128],
+               T[x][:, a:a + n], T[x + "s"][:, a:a + n], True, True)
+        readers[b] = []
+        return t
+
+    def rd(b, t):
+        readers[b].append(t)
+        return t
+
+    def quant(q, a, tile, b, n, deps):
+        return op("v", deps, V.quantize_mx, T[q][:, a:a + n], T[q + "s"][:, a:a + n], T[tile][:, 4 * b:4 * (b + n)])
+
+    def send(k, src, land, d, deps):
+        wait("g", deps)
+        dst = T.cores[me ^ d]
+        rid, pid, _ = topo.addr(dst)
+        m = sum(1 << e for e in topo.engines(core, dst)[:ENGINES[k]])
+        for out, in_ in ((T[land][:, HALF:C].bitcast(dt.uint8), T[src][:, 0:HALF].bitcast(dt.uint8)),
+                         (T[land + "s"][:, HALF:C], T[src + "s"][:, 0:HALF])):
+            g.remote_dma(out_ap=out, in_ap=in_, remote_sem=T.sem["r%d" % k], local_sem=T.sem["l%d" % k],
+                         pid=pid, routing_id=rid, dma_engine_mask=m)
+        return ("r%d" % k, 2 * ENGINES[k]), ("l%d" % k, 2 * ENGINES[k])
+
+    def evac(q, b, out, deps, relu=False, scale=None):
+        src = bank(b)
+        if q == "v":
+            if relu:
+                return rd(b, op("v", deps, V.tensor_scalar, out, src, 0.0, SCALE, A.max, A.mult))
+            if scale:
+                return rd(b, op("v", deps, V.tensor_scalar, out, src, scale, None, A.mult))
+            return rd(b, op("v", deps, V.tensor_copy, out, src))
+        return rd(b, op("a", deps, S.activation, out, src, RELU if relu else COPY, scale=SCALE if relu else (scale or 1.0)))
+
+    d_xu = dma("s", [], (T.xt[:, 4 * HALF:4 * C], T.x[:, 4 * HALF:4 * C]))
+    d_xl = dma("s", [], (T.xt[:, 0:4 * HALF], T.x[:, 0:4 * HALF]))
+    d_u = dma("s", [], (T.ut[:], T.u[:]))
+    d_p = dma("s", [], (T.pt[:, 0:24], T.p0[:]), (T.pt[:, 24:48], T.p1[:]),
+              (T.pt[0:128:2, 48:72], T.p0[1:128:2, :]), (T.pt[1:128:2, 48:72], T.p0[0:128:2, :]),
+              (T.pt[0:128:2, 72:96], T.p1[1:128:2, :]), (T.pt[1:128:2, 72:96], T.p1[0:128:2, :]))
+
+    small = dict(allow_small_or_imprecise_dtypes=True)
+    i_id = op("g", [], g.iota, T.idn[:], [[1, 128]], 0, -1, **small)
+    i_p = op("g", [], g.iota, T.ipp[:], [[1, 1]], 0, 1)
+    i_j8 = op("g", [], g.iota, T.j8[:], [[0, 24], [1, 8]], 0, 0, **small)
+    i_uo = op("g", [], g.iota, T.uoi[:], [[1, 2], [16, 8]], 0, 0)
+    e0 = op("v", [], V.memset, T.eb[:], 0.0)
+    k0 = op("v", [], V.memset, T.keep[:], 1.0)
+    w0 = op("v", [], V.memset, T.w48[:], 0.0)
+    k0 = op("v", [k0], V.memset, T.keep[:, 0:C:16], 0.0)
+    e0 = op("v", [e0, i_id], V.tensor_scalar, T.eb[:, 3:515:4], T.idn[:], 0.0, 0.5, A.is_equal, A.mult)
+    ph = op("v", [i_p], V.tensor_scalar, T.phi[:], T.ipp[:], 15, 1, A.bitwise_and, A.logical_shift_right)
+    uo = op("v", [i_uo], V.tensor_copy, T.uof[:], T.uoi[:])
+    ph = op("v", [ph], V.tensor_copy, T.phf[:], T.phi[:])
+    for b in range(4):
+        eq = op("v", [e0], V.quantize_mx, T.eq[:, 128 * b:128 * b + 128], T.eqs[:, 128 * b:128 * b + 128], T.eb[:, 3 - b:515 - b])
+    op("v", [ph, i_j8], V.tensor_scalar, T.sel[:, 0:C:2], T.j8[:], T.phf[:], None, A.is_equal)
+    sel = op("v", [], V.tensor_scalar, T.sel[:, 1:C:2], T.j8[:], T.phf[:], -1.0, A.is_equal, A.mult)
+
+    xu = quant("su0", 0, "xt", HALF, HALF, [d_xu])
+    r0, l0 = send(0, "su0", "st0", FAR[0], [xu])
+    iot = op("g", [], g.iota, T.iot[:], [[1, C]], 0, 0, **small)
+    d_w = dma("s", [l0], (T.wq[:].bitcast(dt.uint8), T.wc[:]), (T.wqs[:], T.ws[:]))
+    xl = quant("st0", 0, "xt", 0, HALF, [d_xl])
+
+    uq = quant("uq", 0, "ut", 0, 128, [d_u])
+    ups = op("a", [uq, uo], S.activation, T.ups[:], T.uqs[:].indirect(T.uof[:, 0:16]), COPY)
+    up = op("v", [uq, uo], V.tensor_copy, T.up[:].bitcast(dt.uint32), T.uq[:].bitcast(dt.uint32).indirect(T.uof[:, 0:16]))
+
+    def unpack(t, a, banks, deps):
+        return [mm(banks[b], "eq", 128 * b, "st%d" % t, a, HALF, deps) for b in range(4)]
+
+    def unpacked(t, a, banks, ms):
+        return [evac("a", banks[b], T["dd%d" % t][:, C * b + a:C * b + a + HALF], [ms[b]]) for b in range(4)]
+
+    def again(q, t, a, banks, after):
+        return [evac(q, banks[b], T["de%d" % t][:, C * b + a:C * b + a + HALF], [after[b]]) for b in (0, 1)]
+
+    def scores(t, a, b, deps):
+        return mm(b, "up", 128 * t, "st%d" % t, a, HALF, deps)
+
+    def scored(t, a, b, m):
+        return evac("v", b, T["sc%d" % t][:, a:a + HALF], [m])
+
+    dl = unpack(0, 0, (1, 2, 3, 4), [xl, eq])
+    sl = scores(0, 0, 0, [xl, up, ups])
+    ddl = unpacked(0, 0, (1, 2, 3, 4), dl)
+    ddl += again("a", 0, 0, (1, 2, 3, 4), ddl)
+
+    pu = op("v", [d_p], V.tensor_copy, T.pu[:], T.pt[:, 0:48])
+    op("v", [], V.tensor_copy, T.c48[:, 1:96:2], T.pt[:, 0:48])
+    c48 = op("v", [], V.tensor_tensor, T.c48[:, 0:96:2], T.pt[:, 48:96], T.pt[:, 0:48], A.subtract)
+    sl = scored(0, 0, 0, sl)
+    fs = op("v", [], V.tensor_scalar, T.fsh[:], T.pt[:], 4, None, A.logical_shift_right)
+    op("v", [], V.tensor_scalar, T.f24[:], T.pt[:], 24.0, None, A.mult)
+    fs = op("v", [fs], V.tensor_scalar, T.f383[:], T.fsh[:], -383.0, None, A.mult)
+    fs = op("v", [fs], V.tensor_tensor, T.ff[:], T.f24[:], T.f383[:], A.add)
+    op("v", [fs], V.tensor_copy, T.cf[:, 1:96:2], T.ff[:, 0:48])
+    cf = op("v", [fs], V.tensor_tensor, T.cf[:, 0:96:2], T.ff[:, 48:96], T.ff[:, 0:48], A.subtract)
+
+    def lists(t, a, n, deps):
+        sc, m, r, l, lu = T["sc%d" % t], T["mm%d" % t], T["rr%d" % t], T["ll%d" % t], T["lu%d" % t]
+        k, e = a // 16, (a + n) // 16
+        w = 48 * t
+        x = op("v", deps + [pu, sel], V.tensor_tensor, m[:, a:a + n], sc[:, 0:C].indirect(T.pu[:, 24 * t + k:24 * t + e]),
+               T.sel[:, a:a + n], A.mult)
+        x = op("v", [x, k0], V.tensor_tensor_scan, r[:, a:a + n], T.keep[:, a:a + n], m[:, a:a + n], 0.0, A.mult, A.add)
+        x = op("v", [x, w0], V.tensor_scalar, T.w48[:, w + 2 * k + 1:w + 2 * e:2], r[:, a + 15:a + n:16], 0.0, None, A.is_lt)
+        x = op("v", [x, c48], V.tensor_tensor_scan, l[:, 2 * k:2 * e], T.w48[:, w + 2 * k:w + 2 * e],
+               T.c48[:, w + 2 * k:w + 2 * e], 0.0, A.mult, A.add)
+        return op("v", [x], V.tensor_copy, lu[:, k:e], l[:, 2 * k + 1:2 * e:2])
+
+    def places(t):
+        w = 48 * t
+        x = op("v", [cf], V.tensor_tensor_scan, T["lf%d" % t][:], T.w48[:, w:w + 48], T.cf[:, w:w + 48], 0.0, A.mult, A.add)
+        return op("v", [x], V.tensor_copy, T["fu%d" % t][:], T["lf%d" % t][:, 1:48:2])
+
+    def invert(t, deps):
+        inv = T["inv%d" % t]
+        x = op("v", deps + [iot], V.tensor_copy, inv[:, 0:C].indirect(T["fu%d" % t][:, 0:24]), T.iot[:])
+        return dma("s", [x], (T["ivw%d" % t][:], inv[0:128:16, :]))
+
+    def inverse(t, d):
+        return op("v", [d], V.tensor_copy, T["iu%d" % t][:], T["ivw%d" % t][:])
+
+    def write_lists(t, deps):
+        x = op("a", deps + [iot], S.activation, T["lr%d" % t][:], T.iot[:, 0:C].indirect(T["lu%d" % t][:, 0:24]), COPY)
+        dma("s", [x], (T.ol[:, C * t:C * t + C], T["lr%d" % t][0:128:16, :]))
+
+    def pick_mix(t, a, rows, deps, q="a"):
+        lu, tok = T["lu%d" % t][:, a // 16:(a + HALF) // 16], []
+        for b in rows:
+            out, src = T["gt%d" % t][:, C * b + a:C * b + a + HALF], T["dd%d" % t][:, C * b:C * b + C].indirect(lu)
+            tok.append(op("v", deps, V.tensor_copy, out, src) if q == "v" else op("a", deps, S.activation, out, src, COPY))
+        return tok
+
+    def mix_window(t, a, deps):
+        lu = T["lu%d" % t][:, a // 16:(a + HALF) // 16]
+        for b in (0, 1):
+            op("v", deps, V.tensor_tensor, T["pm%d" % t][:, 4 * a + b:4 * (a + HALF):4], T["dd%d" % t][:, C * b:C * b + C].indirect(lu),
+               T["de%d" % t][:, C * b + a:C * b + a + HALF], A.add)
+
+    def mix_bank(t, a, banks, rows, picked):
+        for b, k in zip(rows, picked):
+            x = rd(banks[b], op("v", [k], V.tensor_tensor, T["pm%d" % t][:, 4 * a + b:4 * (a + HALF):4],
+                                T["gt%d" % t][:, C * b + a:C * b + a + HALF], bank(banks[b]), A.add))
+        return x
+
+    def layer(w, x, a, banks, deps):
+        return [mm(banks[b], w, 128 * b, x, a, HALF, deps) for b in range(4)]
+
+    def relus(t, a, banks, ms, who):
+        return [evac(who[b], banks[b], T["hh%d" % t][:, 4 * a + b:4 * (a + HALF):4], [ms[b]], relu=True) for b in range(4)]
+
+    def planes(t, a, banks, ms, who):
+        return [evac(who[b], banks[b], T["gg%d" % t][:, C * b + a:C * b + a + HALF], [ms[b]], scale=SCALE) for b in range(4)]
+
+    def undo(t, a, deps):
+        iu = T["iu%d" % t][:, a // 16:(a + HALF) // 16]
+        tok = []
+        for b, q in enumerate("vvaa"):
+            out, src = T["xx%d" % t][:, 4 * a + b:4 * (a + HALF):4], T["gg%d" % t][:, C * b:C * b + C].indirect(iu)
+            tok.append(op("v", deps, V.tensor_copy, out, src) if q == "v" else op("a", deps, S.activation, out, src, COPY))
+        return tok
+
+    su = scores(0, HALF, 5, [r0, xl, up, ups])
+    du = unpack(0, HALF, (6, 7, 1, 2), [r0, eq])
+    su = scored(0, HALF, 5, su)
+    ddu = unpacked(0, HALF, (6, 7, 1, 2), du)
+    dd0 = ddl + ddu
+    lu = lists(0, HALF, HALF, [sl, su])
+    pk = pick_mix(0, HALF, (1, 2, 3), dd0 + [lu])
+    pk = pick_mix(0, HALF, (0,), dd0 + [lu], "v") + pk
+    x = mix_bank(0, HALF, (6, 7, 1, 2), (0, 1, 2, 3), pk)
+    x = quant("su1", 0, "pm0", HALF, HALF, [x])
+    r1, l1 = send(1, "su1", "qp0", FAR[1], [x])
+    d_z = dma("s", [l1], (T.zq[:].bitcast(dt.uint8), T.zc[:]), (T.zqs[:], T.zs[:]))
+    d_v = dma("s", [], (T.vt[:], T.v[:]))
+    ll = lists(0, 0, HALF, [sl, su])
+    pk = pick_mix(0, 0, (2, 3), dd0 + [ll])
+    mix_window(0, 0, dd0 + [ll])
+    x = mix_bank(0, 0, (1, 2, 3, 4), (2, 3), pk)
+    ql = quant("qp0", 0, "pm0", 0, HALF, [x])
+    ms = layer("wq", "qp0", 0, (0, 5, 6, 7), [ql, d_w])
+    hs = relus(0, 0, (0, 5, 6, 7), ms, "aaaa")
+    d_i0 = invert(0, [places(0)])
+    x = quant("st1", 0, "hh0", 0, HALF, hs)
+    sl = scores(1, 0, 3, [x])
+    dl = unpack(1, 0, (4, 1, 2, 0), [x])
+    sl = scored(1, 0, 3, sl)
+    ddl = unpacked(1, 0, (4, 1, 2, 0), dl)
+    ddl += again("v", 1, 0, (4, 1, 2, 0), ddl)
+
+    ms = layer("wq", "qp0", HALF, (5, 6, 7, 3), [r1, d_w])
+    hs = relus(0, HALF, (5, 6, 7, 3), ms, "avav")
+    x = quant("st1", HALF, "hh0", HALF, HALF, hs)
+    su = scores(1, HALF, 4, [x])
+    du = unpack(1, HALF, (5, 6, 7, 3), [x])
+    su = scored(1, HALF, 4, su)
+    ddu = unpacked(1, HALF, (5, 6, 7, 3), du)
+    again_u = again("a", 1, HALF, (5, 6, 7, 3), ddu)
+    dd1 = ddl + ddu
+    l1st = lists(1, 0, C, [sl, su])
+    pa = pick_mix(1, 0, (2, 3), dd1 + [l1st])
+    pb = pick_mix(1, HALF, (2, 3), dd1 + [l1st])
+    mix_window(1, 0, dd1 + [l1st])
+    x = mix_bank(1, 0, (4, 1, 2, 0), (2, 3), pa)
+    qa = quant("qp1", 0, "pm1", 0, HALF, [x])
+    ma = layer("wq", "qp1", 0, (1, 4, 5, 6), [qa])
+    d_i1 = invert(1, [places(1)])
+    ha = relus(1, 0, (1, 4, 5, 6), ma, "aaaa")
+    mix_window(1, HALF, again_u + [l1st])
+    sa = quant("s2", 0, "hh1", 0, HALF, ha)
+    za = layer("zq", "s2", 0, (1, 4, 2, 0), [sa, d_z])
+    ga = planes(1, 0, (1, 4, 2, 0), za, "aaaa")
+    x = mix_bank(1, HALF, (5, 6, 7, 3), (2, 3), pb)
+    qb = quant("qp1", HALF, "pm1", HALF, HALF, [x])
+    mb = layer("wq", "qp1", HALF, (5, 6, 7, 3), [qb])
+    hb = relus(1, HALF, (5, 6, 7, 3), mb, "avav")
+    sb = quant("s2", HALF, "hh1", HALF, HALF, hb)
+    zb = layer("zq", "s2", HALF, (1, 4, 2, 0), [sb])
+    gb = planes(1, HALF, (1, 4, 2, 0), zb, "avav")
+
+    iu = inverse(1, d_i1)
+    x = undo(1, HALF, ga + gb + [iu])
+    x = quant("bu1", 0, "xx1", HALF, HALF, x)
+    r2, l2 = send(2, "bu1", "sb", FAR[1], [x])
+    x = undo(1, 0, ga + gb + [iu])
+    ql = quant("sb", 0, "xx1", 0, HALF, x)
+    za = layer("zq", "sb", 0, (5, 6, 7, 3), [ql])
+    ga = planes(0, 0, (5, 6, 7, 3), za, "avav")
+    iu = inverse(0, d_i0)
+    vq = quant("vq", 0, "vt", 0, 128, [d_v])
+    write_lists(0, [lu, ll])
+    write_lists(1, [l1st])
+
+    zb = layer("zq", "sb", HALF, (1, 4, 2, 0), [r2])
+    gb = planes(0, HALF, (1, 4, 2, 0), zb, "avav")
+    x = undo(0, HALF, ga + gb + [iu])
+    x = quant("bu0", 0, "xx0", HALF, HALF, x)
+    r3, l3 = send(3, "bu0", "fin", FAR[0], [x])
+    x = undo(0, 0, ga + gb + [iu])
+    ql = quant("fin", 0, "xx0", 0, HALF, x)
+
+    def scales(a):
+        return [(T.osc[4 * k:4 * k + 4, a:a + HALF], T.fins[32 * k:32 * k + 4, a:a + HALF]) for k in range(4)]
+
+    y = mm(5, "vq", 0, "fin", 0, HALF, [ql, vq])
+    y = evac("v", 5, T.yt[:, 0:HALF], [y])
+    dma("s", [ql], (T.oc[:, 0:4 * HALF], T.fin[:, 0:HALF].bitcast(dt.uint8)))
+    dma("a", [ql], *scales(0))
+    dma("s", [y], (T.y[:, 0:HALF], T.yt[:, 0:HALF]))
+    y = mm(6, "vq", 0, "fin", HALF, HALF, [r3])
+    y = evac("v", 6, T.yt[:, HALF:C], [y])
+    dma("s", [r3], (T.oc[:, 4 * HALF:4 * C], T.fin[:, HALF:C].bitcast(dt.uint8)))
+    dma("a", [r3], *scales(HALF))
+    dma("s", [y], (T.y[:, HALF:C], T.yt[:, HALF:C]))
+    wait("s", [("q" + q, n) for q, n in count.items()] + dmas + [r0, r1, r2, r3, l0, l1, l2, l3])

@@ -4,7 +4,7 @@ A = AluOpType
 COPY, RELU = ActivationFunctionType.Copy, ActivationFunctionType.Relu
 C, HALF, FAR = 384, 192, (1, 4)
 SCALE = 0.03125
-ENGINES = (8, 8, 8, 8)
+ENGINES = (16, 8, 8, 16)
 F8, U8, BF, F32, I32, U16 = "float8_e4m3fn_x4", "uint8", "bfloat16", "float32", "int32", "uint16"
 
 SCRATCH = {"ps": ("psum", [128, 4096], F32)}
@@ -29,7 +29,7 @@ _mx(eq=512, uq=128, up=256, vq=128, wq=512, zq=512, fin=C)
 for _t in "01":
     _buf(F32, **{k + _t: n for k, n in dict(sc=C, mm=C, rr=C, ll=48, lf=48, inv=C, ivw=24, lr=C).items()})
     _buf(U16, **{k + _t: 24 for k in ("lu", "fu", "iu")})
-    _buf(BF, **{k + _t: n for k, n in dict(dd=4 * C, de=2 * C, gt=4 * C, pm=4 * C, hh=4 * C, gg=4 * C, xx=4 * C).items()})
+    _buf(BF, **{k + _t: n for k, n in dict(dd=4 * C, gt=4 * C, pm=4 * C, hh=4 * C, gg=4 * C, xx=4 * C).items()})
     _mx(**{k + _t: n for k, n in dict(st=C, qp=C, su=HALF, bu=HALF).items()})
 _mx(sb=C, s2=C)
 
@@ -68,15 +68,16 @@ def rank_program(g, core, T, topo):
         return dmas[-1]
 
     V, S, P = g.vector, g.scalar, g.tensor
-    readers = {b: [] for b in range(8)}
+    readers, written = {b: [] for b in range(8)}, {}
 
-    def bank(b, n=HALF):
-        return T.ps[:, 512 * b:512 * b + n]
+    def bank(b, n=HALF, at=0):
+        return T.ps[:, 512 * b + at:512 * b + at + n]
 
     def mm(b, w, c0, x, a, n, deps):
+        assert readers[b] or b not in written
         t = op("t", deps + readers[b], P.matmul_mx, bank(b, n), T[w][:, c0:c0 + 128], T[w + "s"][:, c0:c0 + 128],
                T[x][:, a:a + n], T[x + "s"][:, a:a + n], True, True)
-        readers[b] = []
+        readers[b], written[b] = [], t
         return t
 
     def rd(b, t):
@@ -90,15 +91,15 @@ def rank_program(g, core, T, topo):
         wait("g", deps)
         dst = T.cores[me ^ d]
         rid, pid, _ = topo.addr(dst)
-        m = sum(1 << e for e in topo.engines(core, dst)[:ENGINES[k]])
+        e = topo.engines(core, dst)[:ENGINES[k]]
         for out, in_ in ((T[land][:, HALF:C].bitcast(dt.uint8), T[src][:, 0:HALF].bitcast(dt.uint8)),
                          (T[land + "s"][:, HALF:C], T[src + "s"][:, 0:HALF])):
             g.remote_dma(out_ap=out, in_ap=in_, remote_sem=T.sem["r%d" % k], local_sem=T.sem["l%d" % k],
-                         pid=pid, routing_id=rid, dma_engine_mask=m)
-        return ("r%d" % k, 2 * ENGINES[k]), ("l%d" % k, 2 * ENGINES[k])
+                         pid=pid, routing_id=rid, dma_engine_mask=sum(1 << i for i in e))
+        return ("r%d" % k, 2 * len(e)), ("l%d" % k, 2 * len(e))
 
-    def evac(q, b, out, deps, relu=False, scale=None):
-        src = bank(b)
+    def evac(q, b, out, deps, relu=False, scale=None, n=HALF):
+        src = bank(b, n)
         if q == "v":
             if relu:
                 return rd(b, op("v", deps, V.tensor_scalar, out, src, 0.0, SCALE, A.max, A.mult))
@@ -108,11 +109,11 @@ def rank_program(g, core, T, topo):
         return rd(b, op("a", deps, S.activation, out, src, RELU if relu else COPY, scale=SCALE if relu else (scale or 1.0)))
 
     d_xu = dma("s", [], (T.xt[:, 4 * HALF:4 * C], T.x[:, 4 * HALF:4 * C]))
-    d_xl = dma("s", [], (T.xt[:, 0:4 * HALF], T.x[:, 0:4 * HALF]))
-    d_u = dma("s", [], (T.ut[:], T.u[:]))
     d_p = dma("s", [], (T.pt[:, 0:24], T.p0[:]), (T.pt[:, 24:48], T.p1[:]),
               (T.pt[0:128:2, 48:72], T.p0[1:128:2, :]), (T.pt[1:128:2, 48:72], T.p0[0:128:2, :]),
               (T.pt[0:128:2, 72:96], T.p1[1:128:2, :]), (T.pt[1:128:2, 72:96], T.p1[0:128:2, :]))
+    d_xl = dma("s", [], (T.xt[:, 0:4 * HALF], T.x[:, 0:4 * HALF]))
+    d_u = dma("s", [], (T.ut[:], T.u[:]))
 
     small = dict(allow_small_or_imprecise_dtypes=True)
     i_id = op("g", [], g.iota, T.idn[:], [[1, 128]], 0, -1, **small)
@@ -136,49 +137,44 @@ def rank_program(g, core, T, topo):
     r0, l0 = send(0, "su0", "st0", FAR[0], [xu])
     iot = op("g", [], g.iota, T.iot[:], [[1, C]], 0, 0, **small)
     d_w = dma("s", [l0], (T.wq[:].bitcast(dt.uint8), T.wc[:]), (T.wqs[:], T.ws[:]))
+
+    pu = op("v", [d_p], V.tensor_copy, T.pu[:], T.pt[:, 0:48])
+    op("v", [], V.tensor_copy, T.c48[:, 1:96:2], T.pt[:, 0:48])
+    c48 = op("v", [], V.tensor_tensor, T.c48[:, 0:96:2], T.pt[:, 48:96], T.pt[:, 0:48], A.subtract)
+    fs = op("v", [], V.tensor_scalar, T.fsh[:], T.pt[:], 4, None, A.logical_shift_right)
+    op("v", [], V.tensor_scalar, T.f24[:], T.pt[:], 24.0, None, A.mult)
     xl = quant("st0", 0, "xt", 0, HALF, [d_xl])
 
     uq = quant("uq", 0, "ut", 0, 128, [d_u])
     ups = op("a", [uq, uo], S.activation, T.ups[:], T.uqs[:].indirect(T.uof[:, 0:16]), COPY)
     up = op("v", [uq, uo], V.tensor_copy, T.up[:].bitcast(dt.uint32), T.uq[:].bitcast(dt.uint32).indirect(T.uof[:, 0:16]))
 
-    def unpack(t, a, banks, deps):
-        return [mm(banks[b], "eq", 128 * b, "st%d" % t, a, HALF, deps) for b in range(4)]
-
-    def unpacked(t, a, banks, ms):
-        return [evac("a", banks[b], T["dd%d" % t][:, C * b + a:C * b + a + HALF], [ms[b]]) for b in range(4)]
-
-    def again(q, t, a, banks, after):
-        return [evac(q, banks[b], T["de%d" % t][:, C * b + a:C * b + a + HALF], [after[b]]) for b in (0, 1)]
-
-    def scores(t, a, b, deps):
-        return mm(b, "up", 128 * t, "st%d" % t, a, HALF, deps)
-
-    def scored(t, a, b, m):
-        return evac("v", b, T["sc%d" % t][:, a:a + HALF], [m])
-
-    dl = unpack(0, 0, (1, 2, 3, 4), [xl, eq])
-    sl = scores(0, 0, 0, [xl, up, ups])
-    ddl = unpacked(0, 0, (1, 2, 3, 4), dl)
-    ddl += again("a", 0, 0, (1, 2, 3, 4), ddl)
-
-    pu = op("v", [d_p], V.tensor_copy, T.pu[:], T.pt[:, 0:48])
-    op("v", [], V.tensor_copy, T.c48[:, 1:96:2], T.pt[:, 0:48])
-    c48 = op("v", [], V.tensor_tensor, T.c48[:, 0:96:2], T.pt[:, 48:96], T.pt[:, 0:48], A.subtract)
-    sl = scored(0, 0, 0, sl)
-    fs = op("v", [], V.tensor_scalar, T.fsh[:], T.pt[:], 4, None, A.logical_shift_right)
-    op("v", [], V.tensor_scalar, T.f24[:], T.pt[:], 24.0, None, A.mult)
     fs = op("v", [fs], V.tensor_scalar, T.f383[:], T.fsh[:], -383.0, None, A.mult)
     fs = op("v", [fs], V.tensor_tensor, T.ff[:], T.f24[:], T.f383[:], A.add)
     op("v", [fs], V.tensor_copy, T.cf[:, 1:96:2], T.ff[:, 0:48])
     cf = op("v", [fs], V.tensor_tensor, T.cf[:, 0:96:2], T.ff[:, 48:96], T.ff[:, 0:48], A.subtract)
 
-    def lists(t, a, n, deps):
-        sc, m, r, l, lu = T["sc%d" % t], T["mm%d" % t], T["rr%d" % t], T["ll%d" % t], T["lu%d" % t]
+    def unpack(t, a, n, banks, deps):
+        return [mm(banks[b], "eq", 128 * b, "st%d" % t, a, n, deps) for b in range(4)]
+
+    def unpacked(t, a, n, banks, ms, who="aaaa"):
+        return [evac(who[b], banks[b], T["dd%d" % t][:, C * b + a:C * b + a + n], [ms[b]], n=n) for b in range(4)]
+
+    def scores(t, a, b, deps):
+        return mm(b, "up", 128 * t, "st%d" % t, a, HALF, deps)
+
+    def scored(t, a, b, m, q="v"):
+        return evac(q, b, T["sc%d" % t][:, a:a + HALF], [m])
+
+    def contend(t, a, n, deps):
+        k, e = a // 16, (a + n) // 16
+        return op("v", deps + [pu, sel], V.tensor_tensor, T["mm%d" % t][:, a:a + n],
+                  T["sc%d" % t][:, 0:C].indirect(T.pu[:, 24 * t + k:24 * t + e]), T.sel[:, a:a + n], A.mult)
+
+    def lists(t, a, n, x):
+        m, r, l, lu = T["mm%d" % t], T["rr%d" % t], T["ll%d" % t], T["lu%d" % t]
         k, e = a // 16, (a + n) // 16
         w = 48 * t
-        x = op("v", deps + [pu, sel], V.tensor_tensor, m[:, a:a + n], sc[:, 0:C].indirect(T.pu[:, 24 * t + k:24 * t + e]),
-               T.sel[:, a:a + n], A.mult)
         x = op("v", [x, k0], V.tensor_tensor_scan, r[:, a:a + n], T.keep[:, a:a + n], m[:, a:a + n], 0.0, A.mult, A.add)
         x = op("v", [x, w0], V.tensor_scalar, T.w48[:, w + 2 * k + 1:w + 2 * e:2], r[:, a + 15:a + n:16], 0.0, None, A.is_lt)
         x = op("v", [x, c48], V.tensor_tensor_scan, l[:, 2 * k:2 * e], T.w48[:, w + 2 * k:w + 2 * e],
@@ -198,9 +194,12 @@ def rank_program(g, core, T, topo):
     def inverse(t, d):
         return op("v", [d], V.tensor_copy, T["iu%d" % t][:], T["ivw%d" % t][:])
 
-    def write_lists(t, deps):
-        x = op("a", deps + [iot], S.activation, T["lr%d" % t][:], T.iot[:, 0:C].indirect(T["lu%d" % t][:, 0:24]), COPY)
-        dma("s", [x], (T.ol[:, C * t:C * t + C], T["lr%d" % t][0:128:16, :]))
+    def write_lists(q, t, deps):
+        out, src = T["lr%d" % t][:], T.iot[:, 0:C].indirect(T["lu%d" % t][:, 0:24])
+        return op("v", deps + [iot], V.tensor_copy, out, src) if q == "v" else op("a", deps + [iot], S.activation, out, src, COPY)
+
+    def store_lists(t, x):
+        dma("a", [x], (T.ol[:, C * t:C * t + C], T["lr%d" % t][0:128:16, :]))
 
     def pick_mix(t, a, rows, deps, q="a"):
         lu, tok = T["lu%d" % t][:, a // 16:(a + HALF) // 16], []
@@ -209,16 +208,10 @@ def rank_program(g, core, T, topo):
             tok.append(op("v", deps, V.tensor_copy, out, src) if q == "v" else op("a", deps, S.activation, out, src, COPY))
         return tok
 
-    def mix_window(t, a, deps):
-        lu = T["lu%d" % t][:, a // 16:(a + HALF) // 16]
-        for b in (0, 1):
-            op("v", deps, V.tensor_tensor, T["pm%d" % t][:, 4 * a + b:4 * (a + HALF):4], T["dd%d" % t][:, C * b:C * b + C].indirect(lu),
-               T["de%d" % t][:, C * b + a:C * b + a + HALF], A.add)
-
-    def mix_bank(t, a, banks, rows, picked):
+    def mix(t, a, banks, rows, picked, at=0):
         for b, k in zip(rows, picked):
-            x = rd(banks[b], op("v", [k], V.tensor_tensor, T["pm%d" % t][:, 4 * a + b:4 * (a + HALF):4],
-                                T["gt%d" % t][:, C * b + a:C * b + a + HALF], bank(banks[b]), A.add))
+            x = rd(banks[b], op("v", [k, written[banks[b]]], V.tensor_tensor, T["pm%d" % t][:, 4 * a + b:4 * (a + HALF):4],
+                                T["gt%d" % t][:, C * b + a:C * b + a + HALF], bank(banks[b], at=at), A.add))
         return x
 
     def layer(w, x, a, banks, deps):
@@ -230,91 +223,91 @@ def rank_program(g, core, T, topo):
     def planes(t, a, banks, ms, who):
         return [evac(who[b], banks[b], T["gg%d" % t][:, C * b + a:C * b + a + HALF], [ms[b]], scale=SCALE) for b in range(4)]
 
-    def undo(t, a, deps):
-        iu = T["iu%d" % t][:, a // 16:(a + HALF) // 16]
-        tok = []
-        for b, q in enumerate("vvaa"):
-            out, src = T["xx%d" % t][:, 4 * a + b:4 * (a + HALF):4], T["gg%d" % t][:, C * b:C * b + C].indirect(iu)
+    def undo(t, a, gl, gu, iu, who):
+        lst, tok = T["iu%d" % t][:, a // 16:(a + HALF) // 16], []
+        for b, q in enumerate(who):
+            out, src = T["xx%d" % t][:, 4 * a + b:4 * (a + HALF):4], T["gg%d" % t][:, C * b:C * b + C].indirect(lst)
+            deps = [gl[b], gu[b], iu]
             tok.append(op("v", deps, V.tensor_copy, out, src) if q == "v" else op("a", deps, S.activation, out, src, COPY))
         return tok
 
-    su = scores(0, HALF, 5, [r0, xl, up, ups])
-    du = unpack(0, HALF, (6, 7, 1, 2), [r0, eq])
-    su = scored(0, HALF, 5, su)
-    ddu = unpacked(0, HALF, (6, 7, 1, 2), du)
+    sl = scores(0, 0, 4, [xl, up, ups])
+    dl = unpack(0, 0, HALF, (0, 1, 2, 3), [xl, eq])
+    sl = scored(0, 0, 4, sl)
+    ddl = unpacked(0, 0, HALF, (0, 1, 2, 3), dl)
+
+    su = scores(0, HALF, 4, [r0, xl, up, ups])
+    su = scored(0, HALF, 4, su)
+    du = unpack(0, HALF, HALF, (5, 6, 7, 4), [r0, eq])
+    ddu = unpacked(0, HALF, HALF, (5, 6, 7, 4), du)
     dd0 = ddl + ddu
-    lu = lists(0, HALF, HALF, [sl, su])
-    pk = pick_mix(0, HALF, (1, 2, 3), dd0 + [lu])
-    pk = pick_mix(0, HALF, (0,), dd0 + [lu], "v") + pk
-    x = mix_bank(0, HALF, (6, 7, 1, 2), (0, 1, 2, 3), pk)
+    lu = lists(0, HALF, HALF, contend(0, HALF, HALF, [sl, su]))
+    pa = pick_mix(0, HALF, (1, 2, 3), dd0 + [lu])
+    pv = pick_mix(0, HALF, (0,), dd0 + [lu], "v")
+    mix(0, HALF, (5, 6, 7, 4), (0,), pv)
+    cl = contend(0, 0, HALF, [sl, su])
+    x = mix(0, HALF, (5, 6, 7, 4), (1, 2, 3), pa)
     x = quant("su1", 0, "pm0", HALF, HALF, [x])
     r1, l1 = send(1, "su1", "qp0", FAR[1], [x])
     d_z = dma("s", [l1], (T.zq[:].bitcast(dt.uint8), T.zc[:]), (T.zqs[:], T.zs[:]))
     d_v = dma("s", [], (T.vt[:], T.v[:]))
-    ll = lists(0, 0, HALF, [sl, su])
-    pk = pick_mix(0, 0, (2, 3), dd0 + [ll])
-    mix_window(0, 0, dd0 + [ll])
-    x = mix_bank(0, 0, (1, 2, 3, 4), (2, 3), pk)
+    ll = lists(0, 0, HALF, cl)
+    pa = pick_mix(0, 0, (1, 2, 3), dd0 + [ll])
+    pv = pick_mix(0, 0, (0,), dd0 + [ll], "v")
+    mix(0, 0, (0, 1, 2, 3), (0,), pv)
+    f0 = places(0)
+    x = mix(0, 0, (0, 1, 2, 3), (1, 2, 3), pa)
     ql = quant("qp0", 0, "pm0", 0, HALF, [x])
-    ms = layer("wq", "qp0", 0, (0, 5, 6, 7), [ql, d_w])
-    hs = relus(0, 0, (0, 5, 6, 7), ms, "aaaa")
-    d_i0 = invert(0, [places(0)])
-    x = quant("st1", 0, "hh0", 0, HALF, hs)
-    sl = scores(1, 0, 3, [x])
-    dl = unpack(1, 0, (4, 1, 2, 0), [x])
-    sl = scored(1, 0, 3, sl)
-    ddl = unpacked(1, 0, (4, 1, 2, 0), dl)
-    ddl += again("v", 1, 0, (4, 1, 2, 0), ddl)
+    ms = layer("wq", "qp0", 0, (4, 5, 6, 7), [ql, d_w])
+    hs = relus(0, 0, (4, 5, 6, 7), ms, "avav")
+    hl = quant("st1", 0, "hh0", 0, HALF, hs)
 
-    ms = layer("wq", "qp0", HALF, (5, 6, 7, 3), [r1, d_w])
-    hs = relus(0, HALF, (5, 6, 7, 3), ms, "avav")
-    x = quant("st1", HALF, "hh0", HALF, HALF, hs)
-    su = scores(1, HALF, 4, [x])
-    du = unpack(1, HALF, (5, 6, 7, 3), [x])
-    su = scored(1, HALF, 4, su)
-    ddu = unpacked(1, HALF, (5, 6, 7, 3), du)
-    again_u = again("a", 1, HALF, (5, 6, 7, 3), ddu)
-    dd1 = ddl + ddu
-    l1st = lists(1, 0, C, [sl, su])
-    pa = pick_mix(1, 0, (2, 3), dd1 + [l1st])
-    pb = pick_mix(1, HALF, (2, 3), dd1 + [l1st])
-    mix_window(1, 0, dd1 + [l1st])
-    x = mix_bank(1, 0, (4, 1, 2, 0), (2, 3), pa)
-    qa = quant("qp1", 0, "pm1", 0, HALF, [x])
-    ma = layer("wq", "qp1", 0, (1, 4, 5, 6), [qa])
+    ms = layer("wq", "qp0", HALF, (0, 1, 2, 3), [r1, d_w])
+    hs = relus(0, HALF, (0, 1, 2, 3), ms, "avav")
+    sl = scores(1, 0, 4, [hl])
+    sl = scored(1, 0, 4, sl, "a")
+    hu = quant("st1", HALF, "hh0", HALF, HALF, hs)
+    su = scores(1, HALF, 0, [hu])
+    dm = unpack(1, 0, C, (5, 6, 7, 4), [hl, hu])
+    su = scored(1, HALF, 0, su)
+    dd1 = unpacked(1, 0, C, (5, 6, 7, 4), dm)
+    l1st = lists(1, 0, C, contend(1, 0, C, [sl, su]))
+    pa = pick_mix(1, 0, (0, 1, 2, 3), dd1 + [l1st])
+    pb = pick_mix(1, HALF, (0, 1, 2, 3), dd1 + [l1st])
     d_i1 = invert(1, [places(1)])
-    ha = relus(1, 0, (1, 4, 5, 6), ma, "aaaa")
-    mix_window(1, HALF, again_u + [l1st])
-    sa = quant("s2", 0, "hh1", 0, HALF, ha)
-    za = layer("zq", "s2", 0, (1, 4, 2, 0), [sa, d_z])
-    ga = planes(1, 0, (1, 4, 2, 0), za, "aaaa")
-    x = mix_bank(1, HALF, (5, 6, 7, 3), (2, 3), pb)
+    x = mix(1, 0, (5, 6, 7, 4), (0, 1, 2, 3), pa)
+    qa = quant("qp1", 0, "pm1", 0, HALF, [x])
+    ma = layer("wq", "qp1", 0, (1, 2, 3, 0), [qa])
+    ha = relus(1, 0, (1, 2, 3, 0), ma, "aaaa")
+    x = mix(1, HALF, (5, 6, 7, 4), (0, 1, 2, 3), pb, HALF)
     qb = quant("qp1", HALF, "pm1", HALF, HALF, [x])
-    mb = layer("wq", "qp1", HALF, (5, 6, 7, 3), [qb])
-    hb = relus(1, HALF, (5, 6, 7, 3), mb, "avav")
+    mb = layer("wq", "qp1", HALF, (5, 6, 7, 4), [qb])
+    sa = quant("s2", 0, "hh1", 0, HALF, ha)
+    za = layer("zq", "s2", 0, (1, 2, 3, 0), [sa, d_z])
+    hb = relus(1, HALF, (5, 6, 7, 4), mb, "vava")
+    ga = planes(1, 0, (1, 2, 3, 0), za, "aaaa")
     sb = quant("s2", HALF, "hh1", HALF, HALF, hb)
-    zb = layer("zq", "s2", HALF, (1, 4, 2, 0), [sb])
-    gb = planes(1, HALF, (1, 4, 2, 0), zb, "avav")
-
+    zb = layer("zq", "s2", HALF, (5, 6, 7, 4), [sb])
+    gb = planes(1, HALF, (5, 6, 7, 4), zb, "vava")
     iu = inverse(1, d_i1)
-    x = undo(1, HALF, ga + gb + [iu])
+
+    x = undo(1, HALF, ga, gb, iu, "vava")
     x = quant("bu1", 0, "xx1", HALF, HALF, x)
     r2, l2 = send(2, "bu1", "sb", FAR[1], [x])
-    x = undo(1, 0, ga + gb + [iu])
+    d_i0 = invert(0, [f0])
+    x = undo(1, 0, ga, gb, iu, "aaaa")
     ql = quant("sb", 0, "xx1", 0, HALF, x)
-    za = layer("zq", "sb", 0, (5, 6, 7, 3), [ql])
-    ga = planes(0, 0, (5, 6, 7, 3), za, "avav")
-    iu = inverse(0, d_i0)
+    za = layer("zq", "sb", 0, (1, 2, 3, 0), [ql])
+    ga = planes(0, 0, (1, 2, 3, 0), za, "avav")
     vq = quant("vq", 0, "vt", 0, 128, [d_v])
-    write_lists(0, [lu, ll])
-    write_lists(1, [l1st])
 
-    zb = layer("zq", "sb", HALF, (1, 4, 2, 0), [r2])
-    gb = planes(0, HALF, (1, 4, 2, 0), zb, "avav")
-    x = undo(0, HALF, ga + gb + [iu])
+    zb = layer("zq", "sb", HALF, (5, 6, 7, 4), [r2])
+    gb = planes(0, HALF, (5, 6, 7, 4), zb, "avav")
+    iu = inverse(0, d_i0)
+    x = undo(0, HALF, ga, gb, iu, "avav")
     x = quant("bu0", 0, "xx0", HALF, HALF, x)
     r3, l3 = send(3, "bu0", "fin", FAR[0], [x])
-    x = undo(0, 0, ga + gb + [iu])
+    x = undo(0, 0, ga, gb, iu, "avav")
     ql = quant("fin", 0, "xx0", 0, HALF, x)
 
     def scales(a):
@@ -323,7 +316,11 @@ def rank_program(g, core, T, topo):
     y = mm(5, "vq", 0, "fin", 0, HALF, [ql, vq])
     y = evac("v", 5, T.yt[:, 0:HALF], [y])
     dma("s", [ql], (T.oc[:, 0:4 * HALF], T.fin[:, 0:HALF].bitcast(dt.uint8)))
+    o0 = write_lists("a", 0, [lu, ll])
+    o1 = write_lists("v", 1, [l1st])
     dma("a", [ql], *scales(0))
+    store_lists(0, o0)
+    store_lists(1, o1)
     dma("s", [y], (T.y[:, 0:HALF], T.yt[:, 0:HALF]))
     y = mm(6, "vq", 0, "fin", HALF, HALF, [r3])
     y = evac("v", 6, T.yt[:, HALF:C], [y])

from concourse.mybir import dt, AluOpType, ActivationFunctionType

A = AluOpType
COPY, RELU = ActivationFunctionType.Copy, ActivationFunctionType.Relu
C, HALF, FAR = 384, 192, (1, 4)
SCALE = 0.03125
ENGINES = (16, 8, 8, 16)
F8, U8, BF, F32, I32, U16 = "float8_e4m3fn_x4", "uint8", "bfloat16", "float32", "int32", "uint16"

SCRATCH = {"ps": ("psum", [128, 4096], F32)}


def _buf(dtype, **shapes):
    for k, n in shapes.items():
        SCRATCH[k] = ("sbuf", [128, n], dtype)


def _mx(**widths):
    for k, n in widths.items():
        SCRATCH[k] = ("sbuf", [128, n], F8)
        SCRATCH[k + "s"] = ("sbuf", [128, n], U8)


_buf(BF, xt=4 * C, ut=512, vt=512, eb=520)
_buf(F32, idn=128, j8=HALF, iot=C, phf=1, sel=C, keep=C, w48=96, c48=96, cf=96, f24=96, f383=96, ff=96, yt=C)
_buf(I32, pt=96, ipp=1, phi=1, uoi=16, fsh=96)
_buf(U16, uof=16, pu=48)
_mx(eq=512, uq=128, up=256, vq=128, wq=512, zq=512, fin=C)
for _t in "01":
    _buf(F32, **{k + _t: n for k, n in dict(sc=C, mm=C, rr=C, ll=48, lf=48, inv=C, ivw=24, lr=C).items()})
    _buf(U16, **{k + _t: 24 for k in ("lu", "fu", "iu")})
    _buf(BF, **{k + _t: n for k, n in dict(dd=4 * C, gt=4 * C, pm=4 * C, hh=4 * C, gg=4 * C, xx=4 * C).items()})
    _mx(**{k + _t: n for k, n in dict(st=C, qp=C, su=HALF, bu=HALF).items()})
_mx(sb=C, s2=C)

NDMA = 24
SEMAPHORES = ["qv", "qa", "qt", "qg"] + ["r%d" % k for k in range(4)] + ["l%d" % k for k in range(4)] + ["d%d" % k for k in range(NDMA)]


def rank_program(g, core, T, topo):
    me = T.rank_of(core)
    if me is None:
        return
    queues = {"v": g.vector, "a": g.scalar, "t": g.tensor, "g": g, "s": g.sync}
    count, seen, dmas = {"v": 0, "a": 0, "t": 0, "g": 0}, {}, []

    def wait(q, deps):
        need = {}
        for s, n in deps:
            need[s] = max(n, need.get(s, 0))
        for s, n in need.items():
            if seen.get((q, s), 0) < n:
                queues[q].wait_ge(T.sem[s], n)
                seen[(q, s)] = n

    def op(q, deps, call, *args, **kw):
        wait(q, deps)
        call(*args, **kw).then_inc(T.sem["q" + q], 1)
        count[q] += 1
        return ("q" + q, count[q])

    def dma(q, deps, *moves):
        wait(q, deps)
        s = "d%d" % len(dmas)
        for out, in_ in moves:
            queues[q].dma_start(out, in_).then_inc(T.sem[s], 16)
        dmas.append((s, 16 * len(moves)))
        return dmas[-1]

    V, S, P = g.vector, g.scalar, g.tensor
    readers, written = {b: [] for b in range(8)}, {}

    def bank(b, n=HALF, at=0):
        return T.ps[:, 512 * b + at:512 * b + at + n]

    def mm(b, w, c0, x, a, n, deps):
        assert readers[b] or b not in written
        t = op("t", deps + readers[b], P.matmul_mx, bank(b, n), T[w][:, c0:c0 + 128], T[w + "s"][:, c0:c0 + 128],
               T[x][:, a:a + n], T[x + "s"][:, a:a + n], True, True)
        readers[b], written[b] = [], t
        return t

    def rd(b, t):
        readers[b].append(t)
        return t

    def quant(q, a, tile, b, n, deps):
        return op("v", deps, V.quantize_mx, T[q][:, a:a + n], T[q + "s"][:, a:a + n], T[tile][:, 4 * b:4 * (b + n)])

    def send(k, src, land, d, deps):
        wait("g", deps)
        dst = T.cores[me ^ d]
        rid, pid, _ = topo.addr(dst)
        e = topo.engines(core, dst)[:ENGINES[k]]
        for out, in_ in ((T[land][:, HALF:C].bitcast(dt.uint8), T[src][:, 0:HALF].bitcast(dt.uint8)),
                         (T[land + "s"][:, HALF:C], T[src + "s"][:, 0:HALF])):
            g.remote_dma(out_ap=out, in_ap=in_, remote_sem=T.sem["r%d" % k], local_sem=T.sem["l%d" % k],
                         pid=pid, routing_id=rid, dma_engine_mask=sum(1 << i for i in e))
        return ("r%d" % k, 2 * len(e)), ("l%d" % k, 2 * len(e))

    def evac(q, b, out, deps, relu=False, scale=None, n=HALF):
        src = bank(b, n)
        if q == "v":
            if relu:
                return rd(b, op("v", deps, V.tensor_scalar, out, src, 0.0, SCALE, A.max, A.mult))
            if scale:
                return rd(b, op("v", deps, V.tensor_scalar, out, src, scale, None, A.mult))
            return rd(b, op("v", deps, V.tensor_copy, out, src))
        return rd(b, op("a", deps, S.activation, out, src, RELU if relu else COPY, scale=SCALE if relu else (scale or 1.0)))

    d_xu = dma("s", [], (T.xt[:, 4 * HALF:4 * C], T.x[:, 4 * HALF:4 * C]))
    d_p = dma("s", [], (T.pt[:, 0:24], T.p0[:]), (T.pt[:, 24:48], T.p1[:]),
              (T.pt[0:128:2, 48:72], T.p0[1:128:2, :]), (T.pt[1:128:2, 48:72], T.p0[0:128:2, :]),
              (T.pt[0:128:2, 72:96], T.p1[1:128:2, :]), (T.pt[1:128:2, 72:96], T.p1[0:128:2, :]))
    d_xl = dma("s", [], (T.xt[:, 0:4 * HALF], T.x[:, 0:4 * HALF]))
    d_u = dma("s", [], (T.ut[:], T.u[:]))

    small = dict(allow_small_or_imprecise_dtypes=True)
    i_id = op("g", [], g.iota, T.idn[:], [[1, 128]], 0, -1, **small)
    i_p = op("g", [], g.iota, T.ipp[:], [[1, 1]], 0, 1)
    i_j8 = op("g", [], g.iota, T.j8[:], [[0, 24], [1, 8]], 0, 0, **small)
    i_uo = op("g", [], g.iota, T.uoi[:], [[1, 2], [16, 8]], 0, 0)
    e0 = op("v", [], V.memset, T.eb[:], 0.0)
    k0 = op("v", [], V.memset, T.keep[:], 1.0)
    w0 = op("v", [], V.memset, T.w48[:], 0.0)
    k0 = op("v", [k0], V.memset, T.keep[:, 0:C:16], 0.0)
    e0 = op("v", [e0, i_id], V.tensor_scalar, T.eb[:, 3:515:4], T.idn[:], 0.0, 0.5, A.is_equal, A.mult)
    ph = op("v", [i_p], V.tensor_scalar, T.phi[:], T.ipp[:], 15, 1, A.bitwise_and, A.logical_shift_right)
    uo = op("v", [i_uo], V.tensor_copy, T.uof[:], T.uoi[:])
    ph = op("v", [ph], V.tensor_copy, T.phf[:], T.phi[:])
    for b in range(4):
        eq = op("v", [e0], V.quantize_mx, T.eq[:, 128 * b:128 * b + 128], T.eqs[:, 128 * b:128 * b + 128], T.eb[:, 3 - b:515 - b])
    op("v", [ph, i_j8], V.tensor_scalar, T.sel[:, 0:C:2], T.j8[:], T.phf[:], None, A.is_equal)
    sel = op("v", [], V.tensor_scalar, T.sel[:, 1:C:2], T.j8[:], T.phf[:], -1.0, A.is_equal, A.mult)

    xu = quant("su0", 0, "xt", HALF, HALF, [d_xu])
    r0, l0 = send(0, "su0", "st0", FAR[0], [xu])
    iot = op("g", [], g.iota, T.iot[:], [[1, C]], 0, 0, **small)
    d_w = dma("s", [l0], (T.wq[:].bitcast(dt.uint8), T.wc[:]), (T.wqs[:], T.ws[:]))

    pu = op("v", [d_p], V.tensor_copy, T.pu[:], T.pt[:, 0:48])
    op("v", [], V.tensor_copy, T.c48[:, 1:96:2], T.pt[:, 0:48])
    c48 = op("v", [], V.tensor_tensor, T.c48[:, 0:96:2], T.pt[:, 48:96], T.pt[:, 0:48], A.subtract)
    fs = op("v", [], V.tensor_scalar, T.fsh[:], T.pt[:], 4, None, A.logical_shift_right)
    op("v", [], V.tensor_scalar, T.f24[:], T.pt[:], 24.0, None, A.mult)
    xl = quant("st0", 0, "xt", 0, HALF, [d_xl])

    uq = quant("uq", 0, "ut", 0, 128, [d_u])
    ups = op("a", [uq, uo], S.activation, T.ups[:], T.uqs[:].indirect(T.uof[:, 0:16]), COPY)
    up = op("v", [uq, uo], V.tensor_copy, T.up[:].bitcast(dt.uint32), T.uq[:].bitcast(dt.uint32).indirect(T.uof[:, 0:16]))

    fs = op("v", [fs], V.tensor_scalar, T.f383[:], T.fsh[:], -383.0, None, A.mult)
    fs = op("v", [fs], V.tensor_tensor, T.ff[:], T.f24[:], T.f383[:], A.add)
    op("v", [fs], V.tensor_copy, T.cf[:, 1:96:2], T.ff[:, 0:48])
    cf = op("v", [fs], V.tensor_tensor, T.cf[:, 0:96:2], T.ff[:, 48:96], T.ff[:, 0:48], A.subtract)

    def unpack(t, a, n, banks, deps):
        return [mm(banks[b], "eq", 128 * b, "st%d" % t, a, n, deps) for b in range(4)]

    def unpacked(t, a, n, banks, ms, who="aaaa"):
        return [evac(who[b], banks[b], T["dd%d" % t][:, C * b + a:C * b + a + n], [ms[b]], n=n) for b in range(4)]

    def scores(t, a, b, deps):
        return mm(b, "up", 128 * t, "st%d" % t, a, HALF, deps)

    def scored(t, a, b, m, q="v"):
        return evac(q, b, T["sc%d" % t][:, a:a + HALF], [m])

    def contend(t, a, n, deps):
        k, e = a // 16, (a + n) // 16
        return op("v", deps + [pu, sel], V.tensor_tensor, T["mm%d" % t][:, a:a + n],
                  T["sc%d" % t][:, 0:C].indirect(T.pu[:, 24 * t + k:24 * t + e]), T.sel[:, a:a + n], A.mult)

    def lists(t, a, n, x):
        m, r, l, lu = T["mm%d" % t], T["rr%d" % t], T["ll%d" % t], T["lu%d" % t]
        k, e = a // 16, (a + n) // 16
        w = 48 * t
        x = op("v", [x, k0], V.tensor_tensor_scan, r[:, a:a + n], T.keep[:, a:a + n], m[:, a:a + n], 0.0, A.mult, A.add)
        x = op("v", [x, w0], V.tensor_scalar, T.w48[:, w + 2 * k + 1:w + 2 * e:2], r[:, a + 15:a + n:16], 0.0, None, A.is_lt)
        x = op("v", [x, c48], V.tensor_tensor_scan, l[:, 2 * k:2 * e], T.w48[:, w + 2 * k:w + 2 * e],
               T.c48[:, w + 2 * k:w + 2 * e], 0.0, A.mult, A.add)
        return op("v", [x], V.tensor_copy, lu[:, k:e], l[:, 2 * k + 1:2 * e:2])

    def places(t):
        w = 48 * t
        x = op("v", [cf], V.tensor_tensor_scan, T["lf%d" % t][:], T.w48[:, w:w + 48], T.cf[:, w:w + 48], 0.0, A.mult, A.add)
        return op("v", [x], V.tensor_copy, T["fu%d" % t][:], T["lf%d" % t][:, 1:48:2])

    def invert(t, deps):
        inv = T["inv%d" % t]
        x = op("v", deps + [iot], V.tensor_copy, inv[:, 0:C].indirect(T["fu%d" % t][:, 0:24]), T.iot[:])
        return dma("s", [x], (T["ivw%d" % t][:], inv[0:128:16, :]))

    def inverse(t, d):
        return op("v", [d], V.tensor_copy, T["iu%d" % t][:], T["ivw%d" % t][:])

    def write_lists(q, t, deps):
        out, src = T["lr%d" % t][:], T.iot[:, 0:C].indirect(T["lu%d" % t][:, 0:24])
        return op("v", deps + [iot], V.tensor_copy, out, src) if q == "v" else op("a", deps + [iot], S.activation, out, src, COPY)

    def store_lists(t, x):
        dma("a", [x], (T.ol[:, C * t:C * t + C], T["lr%d" % t][0:128:16, :]))

    def pick_mix(t, a, rows, deps, q="a"):
        lu, tok = T["lu%d" % t][:, a // 16:(a + HALF) // 16], []
        for b in rows:
            out, src = T["gt%d" % t][:, C * b + a:C * b + a + HALF], T["dd%d" % t][:, C * b:C * b + C].indirect(lu)
            tok.append(op("v", deps, V.tensor_copy, out, src) if q == "v" else op("a", deps, S.activation, out, src, COPY))
        return tok

    def mix(t, a, banks, rows, picked, at=0):
        for b, k in zip(rows, picked):
            x = rd(banks[b], op("v", [k, written[banks[b]]], V.tensor_tensor, T["pm%d" % t][:, 4 * a + b:4 * (a + HALF):4],
                                T["gt%d" % t][:, C * b + a:C * b + a + HALF], bank(banks[b], at=at), A.add))
        return x

    def layer(w, x, a, banks, deps):
        return [mm(banks[b], w, 128 * b, x, a, HALF, deps) for b in range(4)]

    def relus(t, a, banks, ms, who):
        return [evac(who[b], banks[b], T["hh%d" % t][:, 4 * a + b:4 * (a + HALF):4], [ms[b]], relu=True) for b in range(4)]

    def planes(t, a, banks, ms, who):
        return [evac(who[b], banks[b], T["gg%d" % t][:, C * b + a:C * b + a + HALF], [ms[b]], scale=SCALE) for b in range(4)]

    def undo(t, a, gl, gu, iu, who):
        lst, tok = T["iu%d" % t][:, a // 16:(a + HALF) // 16], []
        for b, q in enumerate(who):
            out, src = T["xx%d" % t][:, 4 * a + b:4 * (a + HALF):4], T["gg%d" % t][:, C * b:C * b + C].indirect(lst)
            deps = [gl[b], gu[b], iu]
            tok.append(op("v", deps, V.tensor_copy, out, src) if q == "v" else op("a", deps, S.activation, out, src, COPY))
        return tok

    sl = scores(0, 0, 4, [xl, up, ups])
    dl = unpack(0, 0, HALF, (0, 1, 2, 3), [xl, eq])
    sl = scored(0, 0, 4, sl)
    ddl = unpacked(0, 0, HALF, (0, 1, 2, 3), dl)

    su = scores(0, HALF, 4, [r0, xl, up, ups])
    su = scored(0, HALF, 4, su)
    du = unpack(0, HALF, HALF, (5, 6, 7, 4), [r0, eq])
    ddu = unpacked(0, HALF, HALF, (5, 6, 7, 4), du)
    dd0 = ddl + ddu
    lu = lists(0, HALF, HALF, contend(0, HALF, HALF, [sl, su]))
    pa = pick_mix(0, HALF, (1, 2, 3), dd0 + [lu])
    pv = pick_mix(0, HALF, (0,), dd0 + [lu], "v")
    mix(0, HALF, (5, 6, 7, 4), (0,), pv)
    cl = contend(0, 0, HALF, [sl, su])
    x = mix(0, HALF, (5, 6, 7, 4), (1, 2, 3), pa)
    x = quant("su1", 0, "pm0", HALF, HALF, [x])
    r1, l1 = send(1, "su1", "qp0", FAR[1], [x])
    d_z = dma("s", [l1], (T.zq[:].bitcast(dt.uint8), T.zc[:]), (T.zqs[:], T.zs[:]))
    d_v = dma("s", [], (T.vt[:], T.v[:]))
    ll = lists(0, 0, HALF, cl)
    pa = pick_mix(0, 0, (1, 2, 3), dd0 + [ll])
    pv = pick_mix(0, 0, (0,), dd0 + [ll], "v")
    mix(0, 0, (0, 1, 2, 3), (0,), pv)
    f0 = places(0)
    x = mix(0, 0, (0, 1, 2, 3), (1, 2, 3), pa)
    ql = quant("qp0", 0, "pm0", 0, HALF, [x])
    ms = layer("wq", "qp0", 0, (4, 5, 6, 7), [ql, d_w])
    hs = relus(0, 0, (4, 5, 6, 7), ms, "avav")
    hl = quant("st1", 0, "hh0", 0, HALF, hs)

    ms = layer("wq", "qp0", HALF, (0, 1, 2, 3), [r1, d_w])
    hs = relus(0, HALF, (0, 1, 2, 3), ms, "avav")
    sl = scores(1, 0, 4, [hl])
    sl = scored(1, 0, 4, sl, "a")
    hu = quant("st1", HALF, "hh0", HALF, HALF, hs)
    su = scores(1, HALF, 0, [hu])
    dm = unpack(1, 0, C, (5, 6, 7, 4), [hl, hu])
    su = scored(1, HALF, 0, su)
    dd1 = unpacked(1, 0, C, (5, 6, 7, 4), dm)
    l1st = lists(1, 0, C, contend(1, 0, C, [sl, su]))
    pa = pick_mix(1, 0, (0, 1, 2, 3), dd1 + [l1st])
    pb = pick_mix(1, HALF, (0, 1, 2, 3), dd1 + [l1st])
    d_i1 = invert(1, [places(1)])
    x = mix(1, 0, (5, 6, 7, 4), (0, 1, 2, 3), pa)
    qa = quant("qp1", 0, "pm1", 0, HALF, [x])
    ma = layer("wq", "qp1", 0, (1, 2, 3, 0), [qa])
    ha = relus(1, 0, (1, 2, 3, 0), ma, "aaaa")
    x = mix(1, HALF, (5, 6, 7, 4), (0, 1, 2, 3), pb, HALF)
    qb = quant("qp1", HALF, "pm1", HALF, HALF, [x])
    mb = layer("wq", "qp1", HALF, (5, 6, 7, 4), [qb])
    sa = quant("s2", 0, "hh1", 0, HALF, ha)
    za = layer("zq", "s2", 0, (1, 2, 3, 0), [sa, d_z])
    hb = relus(1, HALF, (5, 6, 7, 4), mb, "vava")
    ga = planes(1, 0, (1, 2, 3, 0), za, "aaaa")
    sb = quant("s2", HALF, "hh1", HALF, HALF, hb)
    zb = layer("zq", "s2", HALF, (5, 6, 7, 4), [sb])
    gb = planes(1, HALF, (5, 6, 7, 4), zb, "vava")
    iu = inverse(1, d_i1)

    x = undo(1, HALF, ga, gb, iu, "vava")
    x = quant("bu1", 0, "xx1", HALF, HALF, x)
    r2, l2 = send(2, "bu1", "sb", FAR[1], [x])
    d_i0 = invert(0, [f0])
    x = undo(1, 0, ga, gb, iu, "aaaa")
    ql = quant("sb", 0, "xx1", 0, HALF, x)
    za = layer("zq", "sb", 0, (1, 2, 3, 0), [ql])
    ga = planes(0, 0, (1, 2, 3, 0), za, "avav")
    vq = quant("vq", 0, "vt", 0, 128, [d_v])

    zb = layer("zq", "sb", HALF, (5, 6, 7, 4), [r2])
    gb = planes(0, HALF, (5, 6, 7, 4), zb, "avav")
    iu = inverse(0, d_i0)
    x = undo(0, HALF, ga, gb, iu, "avav")
    x = quant("bu0", 0, "xx0", HALF, HALF, x)
    r3, l3 = send(3, "bu0", "fin", FAR[0], [x])
    x = undo(0, 0, ga, gb, iu, "avav")
    ql = quant("fin", 0, "xx0", 0, HALF, x)

    def scales(a):
        return [(T.osc[4 * k:4 * k + 4, a:a + HALF], T.fins[32 * k:32 * k + 4, a:a + HALF]) for k in range(4)]

    y = mm(5, "vq", 0, "fin", 0, HALF, [ql, vq])
    y = evac("v", 5, T.yt[:, 0:HALF], [y])
    dma("s", [ql], (T.oc[:, 0:4 * HALF], T.fin[:, 0:HALF].bitcast(dt.uint8)))
    o0 = write_lists("a", 0, [lu, ll])
    o1 = write_lists("v", 1, [l1st])
    dma("a", [ql], *scales(0))
    store_lists(0, o0)
    store_lists(1, o1)
    dma("s", [y], (T.y[:, 0:HALF], T.yt[:, 0:HALF]))
    y = mm(6, "vq", 0, "fin", HALF, HALF, [r3])
    y = evac("v", 6, T.yt[:, HALF:C], [y])
    dma("s", [r3], (T.oc[:, 4 * HALF:4 * C], T.fin[:, HALF:C].bitcast(dt.uint8)))
    dma("a", [r3], *scales(HALF))
    dma("s", [y], (T.y[:, HALF:C], T.yt[:, HALF:C]))
    wait("s", [("q" + q, n) for q, n in count.items()] + dmas + [r0, r1, r2, r3, l0, l1, l2, l3])
